import numpy as np
import ml_dtypes

BF16 = ml_dtypes.bfloat16


def bf(x):
    return np.asarray(x, np.float32).astype(BF16)


def f32(x):
    return np.asarray(x, np.float32)


def f64(x):
    return np.asarray(x).astype(np.float64)


def striped(idx):
    return np.tile(idx.reshape(-1, 16).T, (8, 1))


S, K, M, N, E, Q = 256, 256, 384, 192, 1, 192


def setup_inputs():
    return {"base": bf(np.random.standard_normal((M, S))), "x": bf(np.random.standard_normal((K, N))), "w": bf(1.2 * np.random.standard_normal((E, K, M)) / np.sqrt(K)), "s": f32(0.5 + np.random.random_sample((M, 1))), "offs": striped(np.random.permutation(S)[:N])}


def reference(base, x, w, s, offs):
    idx = offs[:16].T.reshape(-1)
    z = f64(base).copy()
    for e in range(E):
        z[:, idx[e * Q : (e + 1) * Q]] += f64(w)[e].T @ f64(x)[:, e * Q : (e + 1) * Q]
    z = z / np.sqrt((z**2).mean(axis=0, keepdims=True) + 1e-5) * f64(s)
    return z

@@ -1,0 +1,76 @@
+import concourse.mybir as mybir
+from concourse.masks import make_identity
+
+P = 128
+S = 256
+K = 256
+M = 384
+N = 192
+KB = K // P
+MB = M // P
+EPS = 1e-5
+
+FLOPS = 2 * K * M * N
+
+BF16, F32, U16 = mybir.dt.bfloat16, mybir.dt.float32, mybir.dt.uint16
+MULT = mybir.AluOpType.mult
+ACT = mybir.ActivationFunctionType
+
+
+def tile_rows_placenorm_base_kernel(tc, base, x, w, s, offs, out):
+    nc = tc.nc
+    with (
+        tc.tile_pool(name="held", bufs=1) as held,
+        tc.psum_pool(name="psum", bufs=1) as psum,
+    ):
+        base_t = held.tile([P, MB, S], BF16, name="base_t")
+        w_t = held.tile([P, KB, M], BF16, name="w_t")
+        x_t = held.tile([P, KB, N], BF16, name="x_t")
+        offsets = held.tile([P, N // 16], U16, name="offsets")
+        gain = held.tile([P, MB], F32, name="gain")
+        nc.sync.dma_start(base_t[:], base.rearrange("(a p) s -> p a s", p=P))
+        nc.sync.dma_start(w_t[:], w.rearrange("e (p b) m -> p (e b) m", b=KB))
+        nc.sync.dma_start(x_t[:], x.rearrange("(p b) n -> p b n", b=KB))
+        nc.sync.dma_start(offsets[:], offs)
+        nc.scalar.dma_start(gain[:], s.rearrange("(a p) o -> p (a o)", p=P))
+
+        ident = held.tile([P, P], BF16, name="ident")
+        ones = held.tile([P, P], BF16, name="ones")
+        eps = held.tile([P, 1], F32, name="eps")
+        nc.vector.memset(eps[:], EPS)
+        nc.vector.memset(ones[:], 1.0)
+        make_identity(nc, ident[:])
+
+        table_warm = held.tile([P, 1], F32, name="table_warm")
+        nc.scalar.activation(table_warm[:], eps[:], ACT.Abs_reciprocal_sqrt)
+
+        windows = [psum.tile([P, S], F32, name=f"window{a}") for a in range(MB)]
+        for a in range(MB):
+            nc.tensor.matmul(windows[a][:], ident[:], base_t[:, a, :], start=True, stop=False)
+
+        for a in range(MB):
+            for b in range(KB):
+                nc.tensor.matmul(
+                    windows[a][:].indirect(offsets[:]),
+                    w_t[:, b, a * P : (a + 1) * P],
+                    x_t[:, b, :],
+                    start=False,
+                    stop=b == KB - 1,
+                )
+
+        square_sum = psum.tile([P, S], F32, name="square_sum")
+        squares = held.tile([P, MB, S], BF16, name="squares")
+        for a in range(MB):
+            nc.scalar.activation(squares[:, a, :], windows[a][:], ACT.Square)
+        for a in range(MB):
+            nc.tensor.matmul(square_sum[:], ones[:], squares[:, a, :], start=a == 0, stop=a == MB - 1)
+
+        rstd = held.tile([P, S], F32, name="rstd")
+        nc.scalar.activation(rstd[:], square_sum[:], ACT.Abs_reciprocal_sqrt, bias=eps[:], scale=1.0 / M)
+
+        result = held.tile([P, MB, S], F32, name="result")
+        for a in range(MB):
+            nc.vector.scalar_tensor_tensor(
+                result[:, a, :], windows[a][:], gain[:, a : a + 1], rstd[:], op0=MULT, op1=MULT
+            )
+            nc.sync.dma_start(out[a * P : (a + 1) * P, :], result[:, a, :])

@@ -9,6 +9,8 @@ N = 192
 KB = K // P
 MB = M // P
 EPS = 1e-5
+WARM_COLUMNS = 512
+WARM_MATMULS = 5
 
 FLOPS = 2 * K * M * N
 
@@ -34,12 +36,18 @@ def tile_rows_placenorm_base_kernel(tc, base, x, w, s, offs, out):
         nc.sync.dma_start(offsets[:], offs)
         nc.scalar.dma_start(gain[:], s.rearrange("(a p) o -> p (a o)", p=P))
 
+        zeros = held.tile([P, WARM_COLUMNS], BF16, name="zeros")
         ident = held.tile([P, P], BF16, name="ident")
         ones = held.tile([P, P], BF16, name="ones")
         eps = held.tile([P, 1], F32, name="eps")
+        nc.vector.memset(zeros[:], 0.0)
         nc.vector.memset(eps[:], EPS)
         nc.vector.memset(ones[:], 1.0)
         make_identity(nc, ident[:])
+
+        spare_bank = psum.tile([P, WARM_COLUMNS], F32, name="spare_bank")
+        for i in range(WARM_MATMULS):
+            nc.tensor.matmul(spare_bank[:], zeros[:, 0:P], zeros[:], start=True, stop=True)
 
         table_warm = held.tile([P, 1], F32, name="table_warm")
         nc.scalar.activation(table_warm[:], eps[:], ACT.Abs_reciprocal_sqrt)

@@ -34,7 +34,6 @@ def tile_rows_placenorm_base_kernel(tc, base, x, w, s, offs, out):
         nc.sync.dma_start(w_t[:], w.rearrange("e (p b) m -> p (e b) m", b=KB))
         nc.sync.dma_start(x_t[:], x.rearrange("(p b) n -> p b n", b=KB))
         nc.sync.dma_start(offsets[:], offs)
-        nc.scalar.dma_start(gain[:], s.rearrange("(a p) o -> p (a o)", p=P))
 
         zeros = held.tile([P, WARM_COLUMNS], BF16, name="zeros")
         ident = held.tile([P, P], BF16, name="ident")
@@ -51,6 +50,8 @@ def tile_rows_placenorm_base_kernel(tc, base, x, w, s, offs, out):
 
         table_warm = held.tile([P, 1], F32, name="table_warm")
         nc.scalar.activation(table_warm[:], eps[:], ACT.Abs_reciprocal_sqrt)
+
+        nc.scalar.dma_start(gain[:], s.rearrange("(a p) o -> p (a o)", p=P))
 
         windows = [psum.tile([P, S], F32, name=f"window{a}") for a in range(MB)]
         for a in range(MB):

@@ -10,7 +10,7 @@ KB = K // P
 MB = M // P
 EPS = 1e-5
 WARM_COLUMNS = 512
-WARM_MATMULS = 5
+WARM_MATMULS = 3
 
 FLOPS = 2 * K * M * N
 

@@ -31,7 +31,7 @@ def tile_rows_placenorm_base_kernel(tc, base, x, w, s, offs, out):
         offsets = held.tile([P, N // 16], U16, name="offsets")
         gain = held.tile([P, MB], F32, name="gain")
         nc.sync.dma_start(base_t[:], base.rearrange("(a p) s -> p a s", p=P))
-        nc.sync.dma_start(w_t[:], w.rearrange("e (p b) m -> p (e b) m", b=KB))
+        nc.scalar.dma_start(w_t[:], w.rearrange("e (p b) m -> p (e b) m", b=KB))
         nc.sync.dma_start(x_t[:], x.rearrange("(p b) n -> p b n", b=KB))
         nc.sync.dma_start(offsets[:], offs)
 

import concourse.mybir as mybir
from concourse.masks import make_identity

P = 128
S = 256
K = 256
M = 384
N = 192
KB = K // P
MB = M // P
EPS = 1e-5
WARM_COLUMNS = 512
WARM_MATMULS = 3

FLOPS = 2 * K * M * N

BF16, F32, U16 = mybir.dt.bfloat16, mybir.dt.float32, mybir.dt.uint16
MULT = mybir.AluOpType.mult
ACT = mybir.ActivationFunctionType


def tile_rows_placenorm_base_kernel(tc, base, x, w, s, offs, out):
    nc = tc.nc
    with (
        tc.tile_pool(name="held", bufs=1) as held,
        tc.psum_pool(name="psum", bufs=1) as psum,
    ):
        base_t = held.tile([P, MB, S], BF16, name="base_t")
        w_t = held.tile([P, KB, M], BF16, name="w_t")
        x_t = held.tile([P, KB, N], BF16, name="x_t")
        offsets = held.tile([P, N // 16], U16, name="offsets")
        gain = held.tile([P, MB], F32, name="gain")
        nc.sync.dma_start(base_t[:], base.rearrange("(a p) s -> p a s", p=P))
        nc.scalar.dma_start(w_t[:], w.rearrange("e (p b) m -> p (e b) m", b=KB))
        nc.sync.dma_start(x_t[:], x.rearrange("(p b) n -> p b n", b=KB))
        nc.sync.dma_start(offsets[:], offs)

        zeros = held.tile([P, WARM_COLUMNS], BF16, name="zeros")
        ident = held.tile([P, P], BF16, name="ident")
        ones = held.tile([P, P], BF16, name="ones")
        eps = held.tile([P, 1], F32, name="eps")
        nc.vector.memset(zeros[:], 0.0)
        nc.vector.memset(eps[:], EPS)
        nc.vector.memset(ones[:], 1.0)
        make_identity(nc, ident[:])

        spare_bank = psum.tile([P, WARM_COLUMNS], F32, name="spare_bank")
        for i in range(WARM_MATMULS):
            nc.tensor.matmul(spare_bank[:], zeros[:, 0:P], zeros[:], start=True, stop=True)

        table_warm = held.tile([P, 1], F32, name="table_warm")
        nc.scalar.activation(table_warm[:], eps[:], ACT.Abs_reciprocal_sqrt)

        nc.scalar.dma_start(gain[:], s.rearrange("(a p) o -> p (a o)", p=P))

        windows = [psum.tile([P, S], F32, name=f"window{a}") for a in range(MB)]
        for a in range(MB):
            nc.tensor.matmul(windows[a][:], ident[:], base_t[:, a, :], start=True, stop=False)

        for a in range(MB):
            for b in range(KB):
                nc.tensor.matmul(
                    windows[a][:].indirect(offsets[:]),
                    w_t[:, b, a * P : (a + 1) * P],
                    x_t[:, b, :],
                    start=False,
                    stop=b == KB - 1,
                )

        square_sum = psum.tile([P, S], F32, name="square_sum")
        squares = held.tile([P, MB, S], BF16, name="squares")
        for a in range(MB):
            nc.scalar.activation(squares[:, a, :], windows[a][:], ACT.Square)
        for a in range(MB):
            nc.tensor.matmul(square_sum[:], ones[:], squares[:, a, :], start=a == 0, stop=a == MB - 1)

        rstd = held.tile([P, S], F32, name="rstd")
        nc.scalar.activation(rstd[:], square_sum[:], ACT.Abs_reciprocal_sqrt, bias=eps[:], scale=1.0 / M)

        result = held.tile([P, MB, S], F32, name="result")
        for a in range(MB):
            nc.vector.scalar_tensor_tensor(
                result[:, a, :], windows[a][:], gain[:, a : a + 1], rstd[:], op0=MULT, op1=MULT
            )
            nc.sync.dma_start(out[a * P : (a + 1) * P, :], result[:, a, :])
